import numpy as np
import ml_dtypes


def mxq(x, axis, fmt="e4m3"):
    dtype, down = {"e4m3": (ml_dtypes.float8_e4m3fn, 7), "e5m2": (ml_dtypes.float8_e5m2, 14)}[fmt]
    v = np.moveaxis(np.asarray(x, np.float32).astype(ml_dtypes.bfloat16).astype(np.float64), axis, -1)
    blocks = v.reshape(v.shape[:-1] + (-1, 32))
    amax = np.abs(blocks).max(-1, keepdims=True)
    byte = np.maximum(np.where(amax > 0, np.frexp(amax)[1] - 1 + 127, 0) - down, 1)
    scale = np.exp2(byte - 127.0)
    codes = (blocks / scale).astype(np.float32).astype(dtype).astype(np.float64)
    return np.moveaxis((codes * scale).reshape(v.shape), -1, axis)


WIDE = False


def mx_kscale(k):
    if not WIDE:
        return np.ones(k)
    levels = np.array([10, -10, 5, -5, 0])
    if k % 512:
        return np.exp2(np.random.permutation(np.resize(levels, k // 32))).repeat(32)
    a = np.empty((k // 512, 16))
    for p in range(k // 512):
        a[p, :8] = np.random.permutation(np.resize(levels, 8))
        for g in range(8):
            far = levels[np.abs(levels - a[p, g]) >= 10]
            a[p, g + 8] = far[np.random.randint(len(far))]
    return np.exp2(a.ravel()).repeat(32)


def f64(x):
    return np.asarray(x).astype(np.float64)


def striped(idx):
    return np.tile(idx.reshape(-1, 16).T, (8, 1)).astype(np.uint16)


def unstriped(offs):
    return offs[:16].T.reshape(-1).astype(np.int64)


def relu(v):
    return np.maximum(v, 0.0)


K, T, S, N, U = 1024, 2048, 512, 128, 1024


def setup_inputs():
    n = np.random.standard_normal
    s = mx_kscale(K)[:, None]
    return {
        "xT": (n((K, T)) * s).astype(np.float32),
        "w1": (n((K, N)) / np.sqrt(K) / s).astype(np.float32),
        "scale": np.random.uniform(0.5, 1.5, (N, U)).astype(np.float32),
        "offs": striped(np.random.permutation(T)[:S]),
        "task": striped(np.random.permutation(U)[(U * np.random.uniform(0, 1, S) ** 4).astype(np.int64)]),
    }


def reference(xT, w1, scale, offs, task):
    xq = mxq(f64(xT)[:, unstriped(offs)], 0, "e4m3")
    y = mxq(f64(w1), 0, "e4m3").T @ xq
    g = f64(scale)[:, unstriped(task)]
    return relu(y * g)

@@ -1,0 +1,107 @@
+from contextlib import ExitStack
+
+import concourse.mybir as mybir
+
+K, T, S, N, U = 1024, 2048, 512, 128, 1024
+FLOPS = 2 * K * N * S
+
+F32 = mybir.dt.float32
+BF16 = mybir.dt.bfloat16
+U32 = mybir.dt.uint32
+U16 = mybir.dt.uint16
+U8 = mybir.dt.uint8
+FP8X4 = mybir.dt.float8_e4m3fn_x4
+ALU = mybir.AluOpType
+
+P = 128
+PACK = 4
+K_PASS = P * PACK
+PASSES = K // K_PASS
+HALF = S // 2
+
+
+def tile_picked_relu_e_kernel(tc, xT, w1, scale, offs, task, out):
+    nc = tc.nc
+    with ExitStack() as ctx:
+        keep = ctx.enter_context(tc.tile_pool(name="keep", bufs=1))
+        psum = ctx.enter_context(tc.psum_pool(name="psum", bufs=1))
+
+        offs_sb = keep.tile([P, S // 16], U16, name="offs_sb")
+        task_sb = keep.tile([P, S // 16], U16, name="task_sb")
+        x_rows = xT.rearrange("(z p j) t -> z j p t", z=PASSES, j=PACK)
+        w_rows = w1.rearrange("(z p j) n -> z p j n", z=PASSES, j=PACK)
+        planes = {}
+        for z in range(PASSES):
+            for j in range(PACK):
+                planes[z, j] = keep.tile([P, T], F32, name="plane_%d_%d" % (z, j))
+                nc.sync.dma_start(out=planes[z, j][:], in_=x_rows[z, j])
+                if (z, j) == (0, 0):
+                    nc.sync.dma_start(offs_sb[:], offs)
+                    nc.sync.dma_start(task_sb[:], task)
+        w_raw = []
+        for z in range(PASSES):
+            w_raw.append(keep.tile([P, PACK, N], F32, name="w_raw_%d" % z))
+            nc.sync.dma_start(out=w_raw[z][:], in_=w_rows[z])
+        scale_sb = keep.tile([P, U], F32, name="scale_sb")
+        nc.sync.dma_start(out=scale_sb[:], in_=scale)
+
+        w_bf = [keep.tile([P, N, PACK], BF16, name="w_bf_%d" % z, tag="w_bf_%d" % z, align_bytes=64) for z in range(PASSES)]
+        w_codes = [keep.tile([P, N], U32, name="w_codes_%d" % z, align_bytes=64) for z in range(PASSES)]
+        w_scales = [keep.tile([P, N], U8, name="w_scales_%d" % z, align_bytes=64) for z in range(PASSES)]
+        x_bf = {}
+        x_codes = {}
+        x_scales = {}
+        for z in range(PASSES):
+            for h in range(2):
+                x_bf[z, h] = keep.tile([P, HALF, PACK], BF16, name="x_bf_%d_%d" % (z, h), align_bytes=64)
+                x_codes[z, h] = keep.tile([P, HALF], U32, name="x_codes_%d_%d" % (z, h), align_bytes=64)
+                x_scales[z, h] = keep.tile([P, HALF], U8, name="x_scales_%d_%d" % (z, h), align_bytes=64)
+
+        def entries(lst, h):
+            return lst[:, h * (HALF // 16) : (h + 1) * (HALF // 16)]
+
+        def gather_x(z, j, h):
+            nc.vector.tensor_copy(x_bf[z, h][:, :, j], planes[z, j][:].indirect(entries(offs_sb, h)))
+
+        def quantize(codes, scales, src):
+            nc.vector.quantize_mx(out=codes[:].bitcast(FP8X4), scales=scales[:], in_=src[:].rearrange("p c j -> p (c j)"))
+
+        for z in range(PASSES):
+            nc.scalar.copy(w_bf[z][:], w_raw[z][:].rearrange("p j n -> p n j"))
+
+        for z in range(PASSES):
+            for j in range(PACK):
+                for h in range(2):
+                    gather_x(z, j, h)
+            if z == 0:
+                for h in range(2):
+                    quantize(x_codes[z, h], x_scales[z, h], x_bf[z, h])
+        quantize(x_codes[1, 0], x_scales[1, 0], x_bf[1, 0])
+        quantize(w_codes[0], w_scales[0], w_bf[0])
+        quantize(x_codes[1, 1], x_scales[1, 1], x_bf[1, 1])
+        quantize(w_codes[1], w_scales[1], w_bf[1])
+
+        acc = [psum.tile([P, 512], F32, name="acc_%d" % h) for h in range(2)]
+        for z in range(PASSES):
+            for h in range(2):
+                nc.tensor.matmul_mx(
+                    out=acc[h][:, :HALF],
+                    lhsT=w_codes[z][:].bitcast(FP8X4),
+                    lhsT_scale=w_scales[z][:],
+                    rhs=x_codes[z, h][:].bitcast(FP8X4),
+                    rhs_scale=x_scales[z, h][:],
+                    start=(z == 0),
+                    stop=(z == PASSES - 1),
+                )
+
+        gate_all = keep.tile([P, S], F32, name="gate", tag="w_bf_1", align_bytes=64)
+        gate = [gate_all[:, h * HALF : (h + 1) * HALF] for h in range(2)]
+        prod = [keep.tile([P, HALF], F32, name="prod_%d" % h) for h in range(2)]
+        res = [keep.tile([P, HALF], F32, name="res_%d" % h) for h in range(2)]
+        for h in range(2):
+            nc.vector.tensor_copy(gate[h], scale_sb[:].indirect(entries(task_sb, h)))
+        for h in range(2):
+            nc.vector.tensor_tensor(prod[h][:], acc[h][:, :HALF], gate[h], ALU.mult)
+        for h in range(2):
+            nc.vector.tensor_scalar_max(res[h][:], prod[h][:], 0.0)
+            nc.sync.dma_start(out=out[:, h * HALF : (h + 1) * HALF], in_=res[h][:])

@@ -40,7 +40,7 @@ def tile_picked_relu_e_kernel(tc, xT, w1, scale, offs, task, out):
                     nc.sync.dma_start(task_sb[:], task)
         w_raw = []
         for z in range(PASSES):
-            w_raw.append(keep.tile([P, PACK, N], F32, name="w_raw_%d" % z))
+            w_raw.append(keep.tile([P, PACK, N], F32, name="w_raw_%d" % z, tag="w_raw_%d" % z, align_bytes=64))
             nc.sync.dma_start(out=w_raw[z][:], in_=w_rows[z])
         scale_sb = keep.tile([P, U], F32, name="scale_sb")
         nc.sync.dma_start(out=scale_sb[:], in_=scale)
@@ -52,9 +52,10 @@ def tile_picked_relu_e_kernel(tc, xT, w1, scale, offs, task, out):
         x_codes = {}
         x_scales = {}
         for z in range(PASSES):
+            codes = keep.tile([P, S], U32, name="x_codes_%d" % z, tag=("x_codes_0", "w_raw_0")[z], align_bytes=64)
             for h in range(2):
                 x_bf[z, h] = keep.tile([P, HALF, PACK], BF16, name="x_bf_%d_%d" % (z, h), align_bytes=64)
-                x_codes[z, h] = keep.tile([P, HALF], U32, name="x_codes_%d_%d" % (z, h), align_bytes=64)
+                x_codes[z, h] = codes[:, h * HALF : (h + 1) * HALF]
                 x_scales[z, h] = keep.tile([P, HALF], U8, name="x_scales_%d_%d" % (z, h), align_bytes=64)
 
         def entries(lst, h):
@@ -64,10 +65,13 @@ def tile_picked_relu_e_kernel(tc, xT, w1, scale, offs, task, out):
             nc.vector.tensor_copy(x_bf[z, h][:, :, j], planes[z, j][:].indirect(entries(offs_sb, h)))
 
         def quantize(codes, scales, src):
-            nc.vector.quantize_mx(out=codes[:].bitcast(FP8X4), scales=scales[:], in_=src[:].rearrange("p c j -> p (c j)"))
+            nc.vector.quantize_mx(out=codes.bitcast(FP8X4), scales=scales[:], in_=src[:].rearrange("p c j -> p (c j)"))
 
         for z in range(PASSES):
-            nc.scalar.copy(w_bf[z][:], w_raw[z][:].rearrange("p j n -> p n j"))
+            nc.scalar.copy(
+                w_bf[z][:].rearrange("p (c i) j -> p c j i", i=4),
+                w_raw[z][:].rearrange("p j (c i) -> p c j i", i=4),
+            )
 
         for z in range(PASSES):
             for j in range(PACK):
@@ -76,10 +80,10 @@ def tile_picked_relu_e_kernel(tc, xT, w1, scale, offs, task, out):
             if z == 0:
                 for h in range(2):
                     quantize(x_codes[z, h], x_scales[z, h], x_bf[z, h])
+        quantize(w_codes[0][:], w_scales[0], w_bf[0])
         quantize(x_codes[1, 0], x_scales[1, 0], x_bf[1, 0])
-        quantize(w_codes[0], w_scales[0], w_bf[0])
         quantize(x_codes[1, 1], x_scales[1, 1], x_bf[1, 1])
-        quantize(w_codes[1], w_scales[1], w_bf[1])
+        quantize(w_codes[1][:], w_scales[1], w_bf[1])
 
         acc = [psum.tile([P, 512], F32, name="acc_%d" % h) for h in range(2)]
         for z in range(PASSES):
@@ -88,13 +92,13 @@ def tile_picked_relu_e_kernel(tc, xT, w1, scale, offs, task, out):
                     out=acc[h][:, :HALF],
                     lhsT=w_codes[z][:].bitcast(FP8X4),
                     lhsT_scale=w_scales[z][:],
-                    rhs=x_codes[z, h][:].bitcast(FP8X4),
+                    rhs=x_codes[z, h].bitcast(FP8X4),
                     rhs_scale=x_scales[z, h][:],
                     start=(z == 0),
                     stop=(z == PASSES - 1),
                 )
 
-        gate_all = keep.tile([P, S], F32, name="gate", tag="w_bf_1", align_bytes=64)
+        gate_all = keep.tile([P, S], F32, name="gate", tag="w_raw_1", align_bytes=64)
         gate = [gate_all[:, h * HALF : (h + 1) * HALF] for h in range(2)]
         prod = [keep.tile([P, HALF], F32, name="prod_%d" % h) for h in range(2)]
         res = [keep.tile([P, HALF], F32, name="res_%d" % h) for h in range(2)]

@@ -30,14 +30,14 @@ def tile_picked_relu_e_kernel(tc, xT, w1, scale, offs, task, out):
         task_sb = keep.tile([P, S // 16], U16, name="task_sb")
         x_rows = xT.rearrange("(z p j) t -> z j p t", z=PASSES, j=PACK)
         w_rows = w1.rearrange("(z p j) n -> z p j n", z=PASSES, j=PACK)
+        nc.sync.dma_start(offs_sb[:], offs)
+        nc.sync.dma_start(task_sb[:], task)
         planes = {}
         for z in range(PASSES):
             for j in range(PACK):
                 planes[z, j] = keep.tile([P, T], F32, name="plane_%d_%d" % (z, j))
-                nc.sync.dma_start(out=planes[z, j][:], in_=x_rows[z, j])
-                if (z, j) == (0, 0):
-                    nc.sync.dma_start(offs_sb[:], offs)
-                    nc.sync.dma_start(task_sb[:], task)
+                queue = nc.scalar if (z, j) == (0, 0) else nc.sync
+                queue.dma_start(out=planes[z, j][:], in_=x_rows[z, j])
         w_raw = []
         for z in range(PASSES):
             w_raw.append(keep.tile([P, PACK, N], F32, name="w_raw_%d" % z, tag="w_raw_%d" % z, align_bytes=64))

@@ -12,18 +12,23 @@ U16 = mybir.dt.uint16
 U8 = mybir.dt.uint8
 FP8X4 = mybir.dt.float8_e4m3fn_x4
 ALU = mybir.AluOpType
+RELU = mybir.ActivationFunctionType.Relu
 
 P = 128
 PACK = 4
 K_PASS = P * PACK
 PASSES = K // K_PASS
 HALF = S // 2
+QUARTER = S // 4
+LAST = 64
+W_BYTES = PACK * N * 4
 
 
 def tile_picked_relu_e_kernel(tc, xT, w1, scale, offs, task, out):
     nc = tc.nc
     with ExitStack() as ctx:
         keep = ctx.enter_context(tc.tile_pool(name="keep", bufs=1))
+        tail = ctx.enter_context(tc.tile_pool(name="tail", bufs=1))
         psum = ctx.enter_context(tc.psum_pool(name="psum", bufs=1))
 
         offs_sb = keep.tile([P, S // 16], U16, name="offs_sb")
@@ -40,7 +45,7 @@ def tile_picked_relu_e_kernel(tc, xT, w1, scale, offs, task, out):
                 queue.dma_start(out=planes[z, j][:], in_=x_rows[z, j])
         w_raw = []
         for z in range(PASSES):
-            w_raw.append(keep.tile([P, PACK, N], F32, name="w_raw_%d" % z, tag="w_raw_%d" % z, align_bytes=64))
+            w_raw.append(tail.tile([P, PACK, N], F32, name="w_raw_%d" % z, offset=z * W_BYTES, align_bytes=64))
             nc.sync.dma_start(out=w_raw[z][:], in_=w_rows[z])
         scale_sb = keep.tile([P, U], F32, name="scale_sb")
         nc.sync.dma_start(out=scale_sb[:], in_=scale)
@@ -52,10 +57,12 @@ def tile_picked_relu_e_kernel(tc, xT, w1, scale, offs, task, out):
         x_codes = {}
         x_scales = {}
         for z in range(PASSES):
-            codes = keep.tile([P, S], U32, name="x_codes_%d" % z, tag=("x_codes_0", "w_raw_0")[z], align_bytes=64)
             for h in range(2):
                 x_bf[z, h] = keep.tile([P, HALF, PACK], BF16, name="x_bf_%d_%d" % (z, h), align_bytes=64)
-                x_codes[z, h] = codes[:, h * HALF : (h + 1) * HALF]
+                if z == 0:
+                    x_codes[z, h] = keep.tile([P, HALF], U32, name="x_codes_%d_%d" % (z, h), align_bytes=64)[:]
+                else:
+                    x_codes[z, h] = tail.tile([P, HALF], U32, name="x_codes_%d_%d" % (z, h), offset=(W_BYTES + 64 - HALF * 4, 0)[h], align_bytes=64)[:]
                 x_scales[z, h] = keep.tile([P, HALF], U8, name="x_scales_%d_%d" % (z, h), align_bytes=64)
 
         def entries(lst, h):
@@ -75,19 +82,19 @@ def tile_picked_relu_e_kernel(tc, xT, w1, scale, offs, task, out):
 
         for z in range(PASSES):
             for j in range(PACK):
-                for h in range(2):
+                for h in (1, 0):
                     gather_x(z, j, h)
             if z == 0:
-                for h in range(2):
+                for h in (1, 0):
                     quantize(x_codes[z, h], x_scales[z, h], x_bf[z, h])
         quantize(w_codes[0][:], w_scales[0], w_bf[0])
-        quantize(x_codes[1, 0], x_scales[1, 0], x_bf[1, 0])
         quantize(x_codes[1, 1], x_scales[1, 1], x_bf[1, 1])
         quantize(w_codes[1][:], w_scales[1], w_bf[1])
+        quantize(x_codes[1, 0], x_scales[1, 0], x_bf[1, 0])
 
         acc = [psum.tile([P, 512], F32, name="acc_%d" % h) for h in range(2)]
         for z in range(PASSES):
-            for h in range(2):
+            for h in (1, 0):
                 nc.tensor.matmul_mx(
                     out=acc[h][:, :HALF],
                     lhsT=w_codes[z][:].bitcast(FP8X4),
@@ -98,14 +105,20 @@ def tile_picked_relu_e_kernel(tc, xT, w1, scale, offs, task, out):
                     stop=(z == PASSES - 1),
                 )
 
-        gate_all = keep.tile([P, S], F32, name="gate", tag="w_raw_1", align_bytes=64)
-        gate = [gate_all[:, h * HALF : (h + 1) * HALF] for h in range(2)]
+        gate = [tail.tile([P, HALF], F32, name="gate_%d" % h, offset=W_BYTES + 64 + h * HALF * 4, align_bytes=64) for h in range(2)]
         prod = [keep.tile([P, HALF], F32, name="prod_%d" % h) for h in range(2)]
         res = [keep.tile([P, HALF], F32, name="res_%d" % h) for h in range(2)]
         for h in range(2):
-            nc.vector.tensor_copy(gate[h], scale_sb[:].indirect(entries(task_sb, h)))
-        for h in range(2):
-            nc.vector.tensor_tensor(prod[h][:], acc[h][:, :HALF], gate[h], ALU.mult)
-        for h in range(2):
-            nc.vector.tensor_scalar_max(res[h][:], prod[h][:], 0.0)
-            nc.sync.dma_start(out=out[:, h * HALF : (h + 1) * HALF], in_=res[h][:])
+            nc.vector.tensor_copy(gate[h][:], scale_sb[:].indirect(entries(task_sb, h)))
+        pieces = ((0, 0, QUARTER), (0, QUARTER, HALF), (1, 0, HALF - LAST), (1, HALF - LAST, HALF))
+        for h, lo, hi in pieces:
+            nc.vector.tensor_tensor(prod[h][:, lo:hi], acc[h][:, lo:hi], gate[h][:, lo:hi], ALU.mult)
+        for h, lo, hi in pieces:
+            if (h, lo) == (0, 0):
+                nc.scalar.activation(res[h][:, lo:hi], prod[h][:, lo:hi], RELU)
+            else:
+                nc.vector.tensor_scalar_max(res[h][:, lo:hi], prod[h][:, lo:hi], 0.0)
+            if h == 0:
+                nc.sync.dma_start(out=out[:, lo:hi], in_=res[h][:, lo:hi])
+            elif hi == HALF:
+                nc.sync.dma_start(out=out[:, HALF:], in_=res[h][:])

@@ -12,14 +12,13 @@ U16 = mybir.dt.uint16
 U8 = mybir.dt.uint8
 FP8X4 = mybir.dt.float8_e4m3fn_x4
 ALU = mybir.AluOpType
-RELU = mybir.ActivationFunctionType.Relu
+COPY = mybir.ActivationFunctionType.Copy
 
 P = 128
 PACK = 4
 K_PASS = P * PACK
 PASSES = K // K_PASS
 HALF = S // 2
-QUARTER = S // 4
 LAST = 64
 W_BYTES = PACK * N * 4
 
@@ -108,17 +107,11 @@ def tile_picked_relu_e_kernel(tc, xT, w1, scale, offs, task, out):
         gate = [tail.tile([P, HALF], F32, name="gate_%d" % h, offset=W_BYTES + 64 + h * HALF * 4, align_bytes=64) for h in range(2)]
         prod = [keep.tile([P, HALF], F32, name="prod_%d" % h) for h in range(2)]
         res = [keep.tile([P, HALF], F32, name="res_%d" % h) for h in range(2)]
-        for h in range(2):
-            nc.vector.tensor_copy(gate[h][:], scale_sb[:].indirect(entries(task_sb, h)))
-        pieces = ((0, 0, QUARTER), (0, QUARTER, HALF), (1, 0, HALF - LAST), (1, HALF - LAST, HALF))
+        for h in (1, 0):
+            nc.scalar.activation(gate[h][:], scale_sb[:].indirect(entries(task_sb, h)), COPY)
+        pieces = ((1, 0, HALF), (0, 0, HALF - LAST), (0, HALF - LAST, HALF))
         for h, lo, hi in pieces:
             nc.vector.tensor_tensor(prod[h][:, lo:hi], acc[h][:, lo:hi], gate[h][:, lo:hi], ALU.mult)
         for h, lo, hi in pieces:
-            if (h, lo) == (0, 0):
-                nc.scalar.activation(res[h][:, lo:hi], prod[h][:, lo:hi], RELU)
-            else:
-                nc.vector.tensor_scalar_max(res[h][:, lo:hi], prod[h][:, lo:hi], 0.0)
-            if h == 0:
-                nc.sync.dma_start(out=out[:, lo:hi], in_=res[h][:, lo:hi])
-            elif hi == HALF:
-                nc.sync.dma_start(out=out[:, HALF:], in_=res[h][:])
+            nc.vector.tensor_scalar_max(res[h][:, lo:hi], prod[h][:, lo:hi], 0.0)
+            nc.sync.dma_start(out=out[:, h * HALF + lo : h * HALF + hi], in_=res[h][:, lo:hi])

@@ -13,14 +13,15 @@ U8 = mybir.dt.uint8
 FP8X4 = mybir.dt.float8_e4m3fn_x4
 ALU = mybir.AluOpType
 COPY = mybir.ActivationFunctionType.Copy
+RELU = mybir.ActivationFunctionType.Relu
 
 P = 128
 PACK = 4
 K_PASS = P * PACK
 PASSES = K // K_PASS
 HALF = S // 2
-LAST = 64
 W_BYTES = PACK * N * 4
+LAST = 64
 
 
 def tile_picked_relu_e_kernel(tc, xT, w1, scale, offs, task, out):
@@ -49,7 +50,7 @@ def tile_picked_relu_e_kernel(tc, xT, w1, scale, offs, task, out):
         scale_sb = keep.tile([P, U], F32, name="scale_sb")
         nc.sync.dma_start(out=scale_sb[:], in_=scale)
 
-        w_bf = [keep.tile([P, N, PACK], BF16, name="w_bf_%d" % z, tag="w_bf_%d" % z, align_bytes=64) for z in range(PASSES)]
+        w_bf = [keep.tile([P, N, PACK], BF16, name="w_bf_%d" % z, align_bytes=64) for z in range(PASSES)]
         w_codes = [keep.tile([P, N], U32, name="w_codes_%d" % z, align_bytes=64) for z in range(PASSES)]
         w_scales = [keep.tile([P, N], U8, name="w_scales_%d" % z, align_bytes=64) for z in range(PASSES)]
         x_bf = {}
@@ -59,59 +60,65 @@ def tile_picked_relu_e_kernel(tc, xT, w1, scale, offs, task, out):
             for h in range(2):
                 x_bf[z, h] = keep.tile([P, HALF, PACK], BF16, name="x_bf_%d_%d" % (z, h), align_bytes=64)
                 if z == 0:
-                    x_codes[z, h] = keep.tile([P, HALF], U32, name="x_codes_%d_%d" % (z, h), align_bytes=64)[:]
+                    x_codes[z, h] = keep.tile([P, HALF], U32, name="x_codes_%d_%d" % (z, h), align_bytes=64)
                 else:
-                    x_codes[z, h] = tail.tile([P, HALF], U32, name="x_codes_%d_%d" % (z, h), offset=(W_BYTES + 64 - HALF * 4, 0)[h], align_bytes=64)[:]
+                    x_codes[z, h] = tail.tile([P, HALF], U32, name="x_codes_%d_%d" % (z, h), offset=h * W_BYTES, align_bytes=64)
                 x_scales[z, h] = keep.tile([P, HALF], U8, name="x_scales_%d_%d" % (z, h), align_bytes=64)
 
-        def entries(lst, h):
-            return lst[:, h * (HALF // 16) : (h + 1) * (HALF // 16)]
-
-        def gather_x(z, j, h):
-            nc.vector.tensor_copy(x_bf[z, h][:, :, j], planes[z, j][:].indirect(entries(offs_sb, h)))
+        def entries(lst, lo, hi):
+            return lst[:, lo // 16 : hi // 16]
 
         def quantize(codes, scales, src):
-            nc.vector.quantize_mx(out=codes.bitcast(FP8X4), scales=scales[:], in_=src[:].rearrange("p c j -> p (c j)"))
+            nc.vector.quantize_mx(out=codes[:].bitcast(FP8X4), scales=scales[:], in_=src[:].rearrange("p c j -> p (c j)"))
 
-        for z in range(PASSES):
-            nc.scalar.copy(
-                w_bf[z][:].rearrange("p (c i) j -> p c j i", i=4),
-                w_raw[z][:].rearrange("p j (c i) -> p c j i", i=4),
-            )
+        def cast_w(copy, z, lo, hi):
+            copy(w_bf[z][:, lo:hi, :].rearrange("p (c i) j -> p c j i", i=4), w_raw[z][:, :, lo:hi].rearrange("p j (c i) -> p c j i", i=4))
 
         for z in range(PASSES):
             for j in range(PACK):
-                for h in (1, 0):
-                    gather_x(z, j, h)
+                window = planes[z, j][:]
+                nc.vector.tensor_copy(x_bf[z, 0][:, :, j], window.indirect(entries(offs_sb, 0, HALF)))
+                if (z, j) != (PASSES - 1, PACK - 1):
+                    nc.vector.tensor_copy(x_bf[z, 1][:, :, j], window.indirect(entries(offs_sb, HALF, S)))
+                else:
+                    dense = keep.tile([P, HALF], BF16, name="dense")
+                    nc.scalar.activation(dense[:], window.indirect(entries(offs_sb, HALF, S)), COPY)
+                    nc.vector.tensor_copy(x_bf[z, 1][:, :, j], dense[:])
             if z == 0:
-                for h in (1, 0):
+                for h in range(2):
                     quantize(x_codes[z, h], x_scales[z, h], x_bf[z, h])
-        quantize(w_codes[0][:], w_scales[0], w_bf[0])
-        quantize(x_codes[1, 1], x_scales[1, 1], x_bf[1, 1])
-        quantize(w_codes[1][:], w_scales[1], w_bf[1])
+
+        cast_w(nc.scalar.copy, 0, 0, N)
+        cast_w(nc.scalar.copy, 1, 0, N // 2)
+        cast_w(nc.vector.tensor_copy, 1, N // 2, N)
+        quantize(w_codes[0], w_scales[0], w_bf[0])
         quantize(x_codes[1, 0], x_scales[1, 0], x_bf[1, 0])
+        quantize(w_codes[1], w_scales[1], w_bf[1])
+        quantize(x_codes[1, 1], x_scales[1, 1], x_bf[1, 1])
 
         acc = [psum.tile([P, 512], F32, name="acc_%d" % h) for h in range(2)]
         for z in range(PASSES):
-            for h in (1, 0):
+            for h in range(2):
                 nc.tensor.matmul_mx(
                     out=acc[h][:, :HALF],
                     lhsT=w_codes[z][:].bitcast(FP8X4),
                     lhsT_scale=w_scales[z][:],
-                    rhs=x_codes[z, h].bitcast(FP8X4),
+                    rhs=x_codes[z, h][:].bitcast(FP8X4),
                     rhs_scale=x_scales[z, h][:],
                     start=(z == 0),
                     stop=(z == PASSES - 1),
                 )
 
-        gate = [tail.tile([P, HALF], F32, name="gate_%d" % h, offset=W_BYTES + 64 + h * HALF * 4, align_bytes=64) for h in range(2)]
+        gate = [keep.tile([P, HALF], F32, name="gate_0"), tail.tile([P, HALF], F32, name="gate_1", offset=W_BYTES + HALF * 4, align_bytes=64)]
         prod = [keep.tile([P, HALF], F32, name="prod_%d" % h) for h in range(2)]
         res = [keep.tile([P, HALF], F32, name="res_%d" % h) for h in range(2)]
-        for h in (1, 0):
-            nc.scalar.activation(gate[h][:], scale_sb[:].indirect(entries(task_sb, h)), COPY)
-        pieces = ((1, 0, HALF), (0, 0, HALF - LAST), (0, HALF - LAST, HALF))
+        nc.scalar.activation(gate[0][:], scale_sb[:].indirect(entries(task_sb, 0, HALF)), COPY)
+        nc.vector.tensor_copy(gate[1][:], scale_sb[:].indirect(entries(task_sb, HALF, S)))
+        pieces = ((0, 0, HALF), (1, 0, HALF - LAST), (1, HALF - LAST, HALF))
         for h, lo, hi in pieces:
             nc.vector.tensor_tensor(prod[h][:, lo:hi], acc[h][:, lo:hi], gate[h][:, lo:hi], ALU.mult)
-        for h, lo, hi in pieces:
+        nc.scalar.activation(res[0][:], prod[0][:], RELU)
+        nc.scalar.dma_start(out=out[:, :HALF], in_=res[0][:])
+        for h, lo, hi in pieces[1:]:
             nc.vector.tensor_scalar_max(res[h][:, lo:hi], prod[h][:, lo:hi], 0.0)
-            nc.sync.dma_start(out=out[:, h * HALF + lo : h * HALF + hi], in_=res[h][:, lo:hi])
+        nc.sync.dma_start(out=out[:, HALF:], in_=res[1][:])

@@ -20,8 +20,10 @@ PACK = 4
 K_PASS = P * PACK
 PASSES = K // K_PASS
 HALF = S // 2
+PIECE = 128
+PIECES = S // PIECE
+X_ON_SCALAR = 192
 W_BYTES = PACK * N * 4
-LAST = 64
 
 
 def tile_picked_relu_e_kernel(tc, xT, w1, scale, offs, task, out):
@@ -53,12 +55,11 @@ def tile_picked_relu_e_kernel(tc, xT, w1, scale, offs, task, out):
         w_bf = [keep.tile([P, N, PACK], BF16, name="w_bf_%d" % z, align_bytes=64) for z in range(PASSES)]
         w_codes = [keep.tile([P, N], U32, name="w_codes_%d" % z, align_bytes=64) for z in range(PASSES)]
         w_scales = [keep.tile([P, N], U8, name="w_scales_%d" % z, align_bytes=64) for z in range(PASSES)]
-        x_bf = {}
+        x_bf = [keep.tile([P, S, PACK], BF16, name="x_bf_%d" % z, align_bytes=64) for z in range(PASSES)]
         x_codes = {}
         x_scales = {}
         for z in range(PASSES):
             for h in range(2):
-                x_bf[z, h] = keep.tile([P, HALF, PACK], BF16, name="x_bf_%d_%d" % (z, h), align_bytes=64)
                 if z == 0:
                     x_codes[z, h] = keep.tile([P, HALF], U32, name="x_codes_%d_%d" % (z, h), align_bytes=64)
                 else:
@@ -69,56 +70,60 @@ def tile_picked_relu_e_kernel(tc, xT, w1, scale, offs, task, out):
             return lst[:, lo // 16 : hi // 16]
 
         def quantize(codes, scales, src):
-            nc.vector.quantize_mx(out=codes[:].bitcast(FP8X4), scales=scales[:], in_=src[:].rearrange("p c j -> p (c j)"))
+            nc.vector.quantize_mx(out=codes[:].bitcast(FP8X4), scales=scales[:], in_=src.rearrange("p c j -> p (c j)"))
 
-        def cast_w(copy, z, lo, hi):
-            copy(w_bf[z][:, lo:hi, :].rearrange("p (c i) j -> p c j i", i=4), w_raw[z][:, :, lo:hi].rearrange("p j (c i) -> p c j i", i=4))
+        def quantize_x(z, h):
+            quantize(x_codes[z, h], x_scales[z, h], x_bf[z][:, h * HALF : (h + 1) * HALF, :])
 
         for z in range(PASSES):
             for j in range(PACK):
                 window = planes[z, j][:]
-                nc.vector.tensor_copy(x_bf[z, 0][:, :, j], window.indirect(entries(offs_sb, 0, HALF)))
-                if (z, j) != (PASSES - 1, PACK - 1):
-                    nc.vector.tensor_copy(x_bf[z, 1][:, :, j], window.indirect(entries(offs_sb, HALF, S)))
-                else:
-                    dense = keep.tile([P, HALF], BF16, name="dense")
-                    nc.scalar.activation(dense[:], window.indirect(entries(offs_sb, HALF, S)), COPY)
-                    nc.vector.tensor_copy(x_bf[z, 1][:, :, j], dense[:])
+                on_vector = S - X_ON_SCALAR if (z, j) == (PASSES - 1, PACK - 1) else S
+                nc.vector.tensor_copy(x_bf[z][:, :on_vector, j], window.indirect(entries(offs_sb, 0, on_vector)))
+                if on_vector < S:
+                    dense = keep.tile([P, X_ON_SCALAR], BF16, name="dense")
+                    nc.scalar.activation(dense[:], window.indirect(entries(offs_sb, on_vector, S)), COPY)
+                    nc.vector.tensor_copy(x_bf[z][:, on_vector:, j], dense[:])
             if z == 0:
                 for h in range(2):
-                    quantize(x_codes[z, h], x_scales[z, h], x_bf[z, h])
+                    quantize_x(z, h)
 
-        cast_w(nc.scalar.copy, 0, 0, N)
-        cast_w(nc.scalar.copy, 1, 0, N // 2)
-        cast_w(nc.vector.tensor_copy, 1, N // 2, N)
-        quantize(w_codes[0], w_scales[0], w_bf[0])
-        quantize(x_codes[1, 0], x_scales[1, 0], x_bf[1, 0])
-        quantize(w_codes[1], w_scales[1], w_bf[1])
-        quantize(x_codes[1, 1], x_scales[1, 1], x_bf[1, 1])
-
-        acc = [psum.tile([P, 512], F32, name="acc_%d" % h) for h in range(2)]
         for z in range(PASSES):
-            for h in range(2):
+            nc.scalar.copy(w_bf[z][:].rearrange("p (c i) j -> p c j i", i=4), w_raw[z][:].rearrange("p j (c i) -> p c j i", i=4))
+        for z in range(PASSES):
+            quantize(w_codes[z], w_scales[z], w_bf[z][:])
+            quantize_x(PASSES - 1, z)
+
+        acc = [psum.tile([P, 512], F32, name="acc_%d" % i) for i in range(PIECES)]
+        for z in range(PASSES):
+            for i in range(PIECES):
+                h, lo = divmod(i * PIECE, HALF)
                 nc.tensor.matmul_mx(
-                    out=acc[h][:, :HALF],
+                    out=acc[i][:, :PIECE],
                     lhsT=w_codes[z][:].bitcast(FP8X4),
                     lhsT_scale=w_scales[z][:],
-                    rhs=x_codes[z, h][:].bitcast(FP8X4),
-                    rhs_scale=x_scales[z, h][:],
+                    rhs=x_codes[z, h][:, lo : lo + PIECE].bitcast(FP8X4),
+                    rhs_scale=x_scales[z, h][:, lo : lo + PIECE],
                     start=(z == 0),
                     stop=(z == PASSES - 1),
                 )
 
-        gate = [keep.tile([P, HALF], F32, name="gate_0"), tail.tile([P, HALF], F32, name="gate_1", offset=W_BYTES + HALF * 4, align_bytes=64)]
-        prod = [keep.tile([P, HALF], F32, name="prod_%d" % h) for h in range(2)]
-        res = [keep.tile([P, HALF], F32, name="res_%d" % h) for h in range(2)]
-        nc.scalar.activation(gate[0][:], scale_sb[:].indirect(entries(task_sb, 0, HALF)), COPY)
-        nc.vector.tensor_copy(gate[1][:], scale_sb[:].indirect(entries(task_sb, HALF, S)))
-        pieces = ((0, 0, HALF), (1, 0, HALF - LAST), (1, HALF - LAST, HALF))
-        for h, lo, hi in pieces:
-            nc.vector.tensor_tensor(prod[h][:, lo:hi], acc[h][:, lo:hi], gate[h][:, lo:hi], ALU.mult)
-        nc.scalar.activation(res[0][:], prod[0][:], RELU)
-        nc.scalar.dma_start(out=out[:, :HALF], in_=res[0][:])
-        for h, lo, hi in pieces[1:]:
-            nc.vector.tensor_scalar_max(res[h][:, lo:hi], prod[h][:, lo:hi], 0.0)
-        nc.sync.dma_start(out=out[:, HALF:], in_=res[1][:])
+        gate = []
+        for i in range(PIECES):
+            looked_up = scale_sb[:].indirect(entries(task_sb, i * PIECE, (i + 1) * PIECE))
+            if i == 1:
+                gate.append(tail.tile([P, PIECE], F32, name="gate_%d" % i, offset=W_BYTES + HALF * 4, align_bytes=64))
+                nc.vector.tensor_copy(gate[i][:], looked_up)
+            else:
+                gate.append(keep.tile([P, PIECE], F32, name="gate_%d" % i))
+                nc.scalar.activation(gate[i][:], looked_up, COPY)
+        prod = keep.tile([P, S], F32, name="prod")
+        res = keep.tile([P, S], F32, name="res")
+        for i in range(PIECES):
+            nc.vector.tensor_tensor(prod[:, i * PIECE : (i + 1) * PIECE], acc[i][:, :PIECE], gate[i][:], ALU.mult)
+        for lo in range(0, HALF, PIECE):
+            nc.scalar.activation(res[:, lo : lo + PIECE], prod[:, lo : lo + PIECE], RELU)
+        nc.scalar.dma_start(out=out[:, :HALF], in_=res[:, :HALF])
+        for lo in range(HALF, S, PIECE):
+            nc.vector.tensor_scalar_max(res[:, lo : lo + PIECE], prod[:, lo : lo + PIECE], 0.0)
+        nc.sync.dma_start(out=out[:, HALF:], in_=res[:, HALF:])

@@ -24,6 +24,7 @@ PIECE = 128
 PIECES = S // PIECE
 X_ON_SCALAR = 192
 W_BYTES = PACK * N * 4
+PAIRS = [(0, 0), (0, 1), (1, 0)]
 
 
 def tile_picked_relu_e_kernel(tc, xT, w1, scale, offs, task, out):
@@ -39,12 +40,18 @@ def tile_picked_relu_e_kernel(tc, xT, w1, scale, offs, task, out):
         w_rows = w1.rearrange("(z p j) n -> z p j n", z=PASSES, j=PACK)
         nc.sync.dma_start(offs_sb[:], offs)
         nc.sync.dma_start(task_sb[:], task)
+        x_pairs = xT.rearrange("(z p u e) t -> z u p e t", z=PASSES, u=2, e=2)
         planes = {}
-        for z in range(PASSES):
-            for j in range(PACK):
-                planes[z, j] = keep.tile([P, T], F32, name="plane_%d_%d" % (z, j))
-                queue = nc.scalar if (z, j) == (0, 0) else nc.sync
-                queue.dma_start(out=planes[z, j][:], in_=x_rows[z, j])
+        for z, u in PAIRS:
+            pair = keep.tile([P, 2, T], F32, name="pair_%d_%d" % (z, u))
+            queue = nc.scalar if (z, u) == PAIRS[0] else nc.sync
+            queue.dma_start(out=pair[:], in_=x_pairs[z, u])
+            for e in range(2):
+                planes[z, 2 * u + e] = pair[:, e, :]
+        for j in range(2, PACK):
+            single = keep.tile([P, T], F32, name="plane_%d" % j)
+            nc.sync.dma_start(out=single[:], in_=x_rows[PASSES - 1, j])
+            planes[PASSES - 1, j] = single[:]
         w_raw = []
         for z in range(PASSES):
             w_raw.append(tail.tile([P, PACK, N], F32, name="w_raw_%d" % z, offset=z * W_BYTES, align_bytes=64))
@@ -76,9 +83,18 @@ def tile_picked_relu_e_kernel(tc, xT, w1, scale, offs, task, out):
             quantize(x_codes[z, h], x_scales[z, h], x_bf[z][:, h * HALF : (h + 1) * HALF, :])
 
         for z in range(PASSES):
-            for j in range(PACK):
-                window = planes[z, j][:]
-                on_vector = S - X_ON_SCALAR if (z, j) == (PASSES - 1, PACK - 1) else S
+            paired = PACK if z == 0 else 2
+            upper = keep.tile([P, paired, HALF], F32, name="upper_%d" % z)
+            for j in range(paired):
+                nc.vector.tensor_copy(x_bf[z][:, :HALF, j], planes[z, j].indirect(entries(offs_sb, 0, HALF)))
+                nc.scalar.activation(upper[:, j, :], planes[z, j].indirect(entries(offs_sb, HALF, S)), COPY)
+            nc.scalar.copy(
+                x_bf[z][:, HALF:, :paired].rearrange("p (c i) j -> p c j i", i=4),
+                upper[:].rearrange("p j (c i) -> p c j i", i=4),
+            )
+            for j in range(paired, PACK):
+                window = planes[z, j]
+                on_vector = S - X_ON_SCALAR if j == PACK - 1 else S
                 nc.vector.tensor_copy(x_bf[z][:, :on_vector, j], window.indirect(entries(offs_sb, 0, on_vector)))
                 if on_vector < S:
                     dense = keep.tile([P, X_ON_SCALAR], BF16, name="dense")

@@ -22,7 +22,7 @@ PASSES = K // K_PASS
 HALF = S // 2
 PIECE = 128
 PIECES = S // PIECE
-X_ON_SCALAR = 192
+X_ON_SCALAR = 256
 W_BYTES = PACK * N * 4
 PAIRS = [(0, 0), (0, 1), (1, 0)]
 

@@ -23,6 +23,8 @@ HALF = S // 2
 PIECE = 128
 PIECES = S // PIECE
 X_ON_SCALAR = 256
+LAST = 64
+FIRST_STORE = 192
 W_BYTES = PACK * N * 4
 PAIRS = [(0, 0), (0, 1), (1, 0)]
 
@@ -124,22 +126,27 @@ def tile_picked_relu_e_kernel(tc, xT, w1, scale, offs, task, out):
                     stop=(z == PASSES - 1),
                 )
 
-        gate = []
-        for i in range(PIECES):
-            looked_up = scale_sb[:].indirect(entries(task_sb, i * PIECE, (i + 1) * PIECE))
-            if i == 1:
-                gate.append(tail.tile([P, PIECE], F32, name="gate_%d" % i, offset=W_BYTES + HALF * 4, align_bytes=64))
-                nc.vector.tensor_copy(gate[i][:], looked_up)
-            else:
-                gate.append(keep.tile([P, PIECE], F32, name="gate_%d" % i))
-                nc.scalar.activation(gate[i][:], looked_up, COPY)
+        gate = keep.tile([P, S], F32, name="gate")
+        gate_v = tail.tile([P, PIECE + LAST], F32, name="gate_v", offset=W_BYTES + HALF * 4, align_bytes=64)
+
+        def looked_up(lo, hi):
+            return scale_sb[:].indirect(entries(task_sb, lo, hi))
+
+        on_scalar = [(0, PIECE), (HALF, HALF + PIECE), (HALF + PIECE, S - LAST)]
+        for lo, hi in on_scalar:
+            nc.scalar.activation(gate[:, lo:hi], looked_up(lo, hi), COPY)
+        nc.vector.tensor_copy(gate_v[:, :PIECE], looked_up(PIECE, HALF))
+        nc.vector.tensor_copy(gate_v[:, PIECE:], looked_up(S - LAST, S))
         prod = keep.tile([P, S], F32, name="prod")
         res = keep.tile([P, S], F32, name="res")
-        for i in range(PIECES):
-            nc.vector.tensor_tensor(prod[:, i * PIECE : (i + 1) * PIECE], acc[i][:, :PIECE], gate[i][:], ALU.mult)
-        for lo in range(0, HALF, PIECE):
-            nc.scalar.activation(res[:, lo : lo + PIECE], prod[:, lo : lo + PIECE], RELU)
-        nc.scalar.dma_start(out=out[:, :HALF], in_=res[:, :HALF])
-        for lo in range(HALF, S, PIECE):
-            nc.vector.tensor_scalar_max(res[:, lo : lo + PIECE], prod[:, lo : lo + PIECE], 0.0)
-        nc.sync.dma_start(out=out[:, HALF:], in_=res[:, HALF:])
+        nc.vector.tensor_tensor(prod[:, :PIECE], acc[0][:, :PIECE], gate[:, :PIECE], ALU.mult)
+        nc.vector.tensor_tensor(prod[:, PIECE:HALF], acc[1][:, :PIECE], gate_v[:, :PIECE], ALU.mult)
+        nc.vector.tensor_tensor(prod[:, HALF : HALF + PIECE], acc[2][:, :PIECE], gate[:, HALF : HALF + PIECE], ALU.mult)
+        nc.vector.tensor_tensor(prod[:, HALF + PIECE : S - LAST], acc[3][:, : PIECE - LAST], gate[:, HALF + PIECE : S - LAST], ALU.mult)
+        nc.vector.tensor_tensor(prod[:, S - LAST :], acc[3][:, PIECE - LAST : PIECE], gate_v[:, PIECE:], ALU.mult)
+        for lo, hi in ((0, PIECE), (PIECE, FIRST_STORE)):
+            nc.scalar.activation(res[:, lo:hi], prod[:, lo:hi], RELU)
+        nc.scalar.dma_start(out=out[:, :FIRST_STORE], in_=res[:, :FIRST_STORE])
+        for lo, hi in ((FIRST_STORE, S - PIECE), (S - PIECE, S)):
+            nc.vector.tensor_scalar_max(res[:, lo:hi], prod[:, lo:hi], 0.0)
+        nc.sync.dma_start(out=out[:, FIRST_STORE:], in_=res[:, FIRST_STORE:])

@@ -106,8 +106,15 @@ def tile_picked_relu_e_kernel(tc, xT, w1, scale, offs, task, out):
                 for h in range(2):
                     quantize_x(z, h)
 
-        for z in range(PASSES):
-            nc.scalar.copy(w_bf[z][:].rearrange("p (c i) j -> p c j i", i=4), w_raw[z][:].rearrange("p j (c i) -> p c j i", i=4))
+        def round_w(copy, z, lo, hi):
+            copy(
+                w_bf[z][:, lo:hi, :].rearrange("p (c i) j -> p c j i", i=4),
+                w_raw[z][:, :, lo:hi].rearrange("p j (c i) -> p c j i", i=4),
+            )
+
+        round_w(nc.scalar.copy, 0, 0, N)
+        round_w(nc.scalar.copy, 1, 0, N // 2)
+        round_w(nc.vector.tensor_copy, 1, N // 2, N)
         for z in range(PASSES):
             quantize(w_codes[z], w_scales[z], w_bf[z][:])
             quantize_x(PASSES - 1, z)

@@ -24,7 +24,6 @@ PIECE = 128
 PIECES = S // PIECE
 X_ON_SCALAR = 256
 LAST = 64
-FIRST_STORE = 192
 W_BYTES = PACK * N * 4
 PAIRS = [(0, 0), (0, 1), (1, 0)]
 
@@ -151,9 +150,10 @@ def tile_picked_relu_e_kernel(tc, xT, w1, scale, offs, task, out):
         nc.vector.tensor_tensor(prod[:, HALF : HALF + PIECE], acc[2][:, :PIECE], gate[:, HALF : HALF + PIECE], ALU.mult)
         nc.vector.tensor_tensor(prod[:, HALF + PIECE : S - LAST], acc[3][:, : PIECE - LAST], gate[:, HALF + PIECE : S - LAST], ALU.mult)
         nc.vector.tensor_tensor(prod[:, S - LAST :], acc[3][:, PIECE - LAST : PIECE], gate_v[:, PIECE:], ALU.mult)
-        for lo, hi in ((0, PIECE), (PIECE, FIRST_STORE)):
-            nc.scalar.activation(res[:, lo:hi], prod[:, lo:hi], RELU)
-        nc.scalar.dma_start(out=out[:, :FIRST_STORE], in_=res[:, :FIRST_STORE])
-        for lo, hi in ((FIRST_STORE, S - PIECE), (S - PIECE, S)):
-            nc.vector.tensor_scalar_max(res[:, lo:hi], prod[:, lo:hi], 0.0)
-        nc.sync.dma_start(out=out[:, FIRST_STORE:], in_=res[:, FIRST_STORE:])
+        for lo in range(0, HALF, PIECE):
+            nc.scalar.activation(res[:, lo : lo + PIECE], prod[:, lo : lo + PIECE], RELU)
+        nc.scalar.dma_start(out=out[:, :PIECE], in_=res[:, :PIECE])
+        nc.sync.dma_start(out=out[:, PIECE:HALF], in_=res[:, PIECE:HALF])
+        for lo in range(HALF, S, PIECE):
+            nc.vector.tensor_scalar_max(res[:, lo : lo + PIECE], prod[:, lo : lo + PIECE], 0.0)
+        nc.sync.dma_start(out=out[:, HALF:], in_=res[:, HALF:])

@@ -24,6 +24,7 @@ PIECE = 128
 PIECES = S // PIECE
 X_ON_SCALAR = 256
 LAST = 64
+W_ON_SCALAR = 96
 W_BYTES = PACK * N * 4
 PAIRS = [(0, 0), (0, 1), (1, 0)]
 
@@ -111,12 +112,17 @@ def tile_picked_relu_e_kernel(tc, xT, w1, scale, offs, task, out):
                 w_raw[z][:, :, lo:hi].rearrange("p j (c i) -> p c j i", i=4),
             )
 
-        round_w(nc.scalar.copy, 0, 0, N)
-        round_w(nc.scalar.copy, 1, 0, N // 2)
-        round_w(nc.vector.tensor_copy, 1, N // 2, N)
+        def gpsimd_round(dst, src):
+            nc.gpsimd.tensor_scalar(dst, src, 1.0, 0.0, ALU.mult, ALU.add)
+
         for z in range(PASSES):
-            quantize(w_codes[z], w_scales[z], w_bf[z][:])
-            quantize_x(PASSES - 1, z)
+            round_w(nc.scalar.copy, z, 0, W_ON_SCALAR)
+        round_w(gpsimd_round, 0, W_ON_SCALAR, N)
+        quantize(w_codes[0], w_scales[0], w_bf[0][:])
+        round_w(nc.vector.tensor_copy, 1, W_ON_SCALAR, N)
+        quantize_x(1, 0)
+        quantize(w_codes[1], w_scales[1], w_bf[1][:])
+        quantize_x(1, 1)
 
         acc = [psum.tile([P, 512], F32, name="acc_%d" % i) for i in range(PIECES)]
         for z in range(PASSES):

@@ -26,7 +26,6 @@ X_ON_SCALAR = 256
 LAST = 64
 W_ON_SCALAR = 96
 W_BYTES = PACK * N * 4
-PAIRS = [(0, 0), (0, 1), (1, 0)]
 
 
 def tile_picked_relu_e_kernel(tc, xT, w1, scale, offs, task, out):
@@ -42,14 +41,13 @@ def tile_picked_relu_e_kernel(tc, xT, w1, scale, offs, task, out):
         w_rows = w1.rearrange("(z p j) n -> z p j n", z=PASSES, j=PACK)
         nc.sync.dma_start(offs_sb[:], offs)
         nc.sync.dma_start(task_sb[:], task)
-        x_pairs = xT.rearrange("(z p u e) t -> z u p e t", z=PASSES, u=2, e=2)
+        x_pass = xT.rearrange("(z p j) t -> z p j t", z=PASSES, j=PACK)
         planes = {}
-        for z, u in PAIRS:
-            pair = keep.tile([P, 2, T], F32, name="pair_%d_%d" % (z, u))
-            queue = nc.scalar if (z, u) == PAIRS[0] else nc.sync
-            queue.dma_start(out=pair[:], in_=x_pairs[z, u])
-            for e in range(2):
-                planes[z, 2 * u + e] = pair[:, e, :]
+        for z, lo, hi, queue in ((0, 0, 1, nc.scalar), (0, 1, PACK, nc.sync), (1, 0, 2, nc.sync)):
+            group = keep.tile([P, hi - lo, T], F32, name="group_%d_%d" % (z, lo))
+            queue.dma_start(out=group[:], in_=x_pass[z][:, lo:hi, :])
+            for j in range(lo, hi):
+                planes[z, j] = group[:, j - lo, :]
         for j in range(2, PACK):
             single = keep.tile([P, T], F32, name="plane_%d" % j)
             nc.sync.dma_start(out=single[:], in_=x_rows[PASSES - 1, j])

@@ -39,13 +39,14 @@ def tile_picked_relu_e_kernel(tc, xT, w1, scale, offs, task, out):
         task_sb = keep.tile([P, S // 16], U16, name="task_sb")
         x_rows = xT.rearrange("(z p j) t -> z j p t", z=PASSES, j=PACK)
         w_rows = w1.rearrange("(z p j) n -> z p j n", z=PASSES, j=PACK)
-        nc.sync.dma_start(offs_sb[:], offs)
-        nc.sync.dma_start(task_sb[:], task)
         x_pass = xT.rearrange("(z p j) t -> z p j t", z=PASSES, j=PACK)
         planes = {}
-        for z, lo, hi, queue in ((0, 0, 1, nc.scalar), (0, 1, PACK, nc.sync), (1, 0, 2, nc.sync)):
+        for z, lo, hi, queue in ((0, 0, 1, nc.sync), (0, 1, 3, nc.scalar), (0, 3, PACK, nc.sync), (1, 0, 2, nc.sync)):
             group = keep.tile([P, hi - lo, T], F32, name="group_%d_%d" % (z, lo))
             queue.dma_start(out=group[:], in_=x_pass[z][:, lo:hi, :])
+            if (z, lo) == (0, 0):
+                nc.sync.dma_start(offs_sb[:], offs)
+                nc.sync.dma_start(task_sb[:], task)
             for j in range(lo, hi):
                 planes[z, j] = group[:, j - lo, :]
         for j in range(2, PACK):

@@ -42,7 +42,7 @@ def tile_picked_relu_e_kernel(tc, xT, w1, scale, offs, task, out):
         x_pass = xT.rearrange("(z p j) t -> z p j t", z=PASSES, j=PACK)
         planes = {}
         for z, lo, hi, queue in ((0, 0, 1, nc.sync), (0, 1, 3, nc.scalar), (0, 3, PACK, nc.sync), (1, 0, 2, nc.sync)):
-            group = keep.tile([P, hi - lo, T], F32, name="group_%d_%d" % (z, lo))
+            group = keep.tile([P, hi - lo, T], F32, name="group_%d_%d" % (z, lo), align_bytes=256)
             queue.dma_start(out=group[:], in_=x_pass[z][:, lo:hi, :])
             if (z, lo) == (0, 0):
                 nc.sync.dma_start(offs_sb[:], offs)
@@ -50,14 +50,14 @@ def tile_picked_relu_e_kernel(tc, xT, w1, scale, offs, task, out):
             for j in range(lo, hi):
                 planes[z, j] = group[:, j - lo, :]
         for j in range(2, PACK):
-            single = keep.tile([P, T], F32, name="plane_%d" % j)
+            single = keep.tile([P, T], F32, name="plane_%d" % j, align_bytes=256)
             nc.sync.dma_start(out=single[:], in_=x_rows[PASSES - 1, j])
             planes[PASSES - 1, j] = single[:]
         w_raw = []
         for z in range(PASSES):
-            w_raw.append(tail.tile([P, PACK, N], F32, name="w_raw_%d" % z, offset=z * W_BYTES, align_bytes=64))
+            w_raw.append(tail.tile([P, PACK, N], F32, name="w_raw_%d" % z, offset=z * W_BYTES, align_bytes=256))
             nc.sync.dma_start(out=w_raw[z][:], in_=w_rows[z])
-        scale_sb = keep.tile([P, U], F32, name="scale_sb")
+        scale_sb = keep.tile([P, U], F32, name="scale_sb", align_bytes=256)
         nc.sync.dma_start(out=scale_sb[:], in_=scale)
 
         w_bf = [keep.tile([P, N, PACK], BF16, name="w_bf_%d" % z, align_bytes=64) for z in range(PASSES)]
@@ -149,7 +149,7 @@ def tile_picked_relu_e_kernel(tc, xT, w1, scale, offs, task, out):
         nc.vector.tensor_copy(gate_v[:, :PIECE], looked_up(PIECE, HALF))
         nc.vector.tensor_copy(gate_v[:, PIECE:], looked_up(S - LAST, S))
         prod = keep.tile([P, S], F32, name="prod")
-        res = keep.tile([P, S], F32, name="res")
+        res = keep.tile([P, S], F32, name="res", align_bytes=256)
         nc.vector.tensor_tensor(prod[:, :PIECE], acc[0][:, :PIECE], gate[:, :PIECE], ALU.mult)
         nc.vector.tensor_tensor(prod[:, PIECE:HALF], acc[1][:, :PIECE], gate_v[:, :PIECE], ALU.mult)
         nc.vector.tensor_tensor(prod[:, HALF : HALF + PIECE], acc[2][:, :PIECE], gate[:, HALF : HALF + PIECE], ALU.mult)

@@ -23,7 +23,6 @@ HALF = S // 2
 PIECE = 128
 PIECES = S // PIECE
 X_ON_SCALAR = 256
-LAST = 64
 W_ON_SCALAR = 96
 W_BYTES = PACK * N * 4
 
@@ -41,9 +40,9 @@ def tile_picked_relu_e_kernel(tc, xT, w1, scale, offs, task, out):
         w_rows = w1.rearrange("(z p j) n -> z p j n", z=PASSES, j=PACK)
         x_pass = xT.rearrange("(z p j) t -> z p j t", z=PASSES, j=PACK)
         planes = {}
-        for z, lo, hi, queue in ((0, 0, 1, nc.sync), (0, 1, 3, nc.scalar), (0, 3, PACK, nc.sync), (1, 0, 2, nc.sync)):
+        for z, lo, hi, queue, row in ((0, 0, 1, nc.sync, None), (0, 3, PACK, nc.scalar, 4096), (0, 1, 3, nc.sync, None), (1, 0, 2, nc.sync, None)):
             group = keep.tile([P, hi - lo, T], F32, name="group_%d_%d" % (z, lo), align_bytes=256)
-            queue.dma_start(out=group[:], in_=x_pass[z][:, lo:hi, :])
+            queue.dma_start(out=group[:], in_=x_pass[z][:, lo:hi, :], max_dma_last_dim=row)
             if (z, lo) == (0, 0):
                 nc.sync.dma_start(offs_sb[:], offs)
                 nc.sync.dma_start(task_sb[:], task)
@@ -138,27 +137,23 @@ def tile_picked_relu_e_kernel(tc, xT, w1, scale, offs, task, out):
                 )
 
         gate = keep.tile([P, S], F32, name="gate")
-        gate_v = tail.tile([P, PIECE + LAST], F32, name="gate_v", offset=W_BYTES + HALF * 4, align_bytes=64)
+        prod = keep.tile([P, S], F32, name="prod")
+        res = keep.tile([P, S], F32, name="res", align_bytes=256)
 
         def looked_up(lo, hi):
             return scale_sb[:].indirect(entries(task_sb, lo, hi))
 
-        on_scalar = [(0, PIECE), (HALF, HALF + PIECE), (HALF + PIECE, S - LAST)]
-        for lo, hi in on_scalar:
+        for lo, hi in ((0, 128), (320, 384), (384, 512)):
             nc.scalar.activation(gate[:, lo:hi], looked_up(lo, hi), COPY)
-        nc.vector.tensor_copy(gate_v[:, :PIECE], looked_up(PIECE, HALF))
-        nc.vector.tensor_copy(gate_v[:, PIECE:], looked_up(S - LAST, S))
-        prod = keep.tile([P, S], F32, name="prod")
-        res = keep.tile([P, S], F32, name="res", align_bytes=256)
-        nc.vector.tensor_tensor(prod[:, :PIECE], acc[0][:, :PIECE], gate[:, :PIECE], ALU.mult)
-        nc.vector.tensor_tensor(prod[:, PIECE:HALF], acc[1][:, :PIECE], gate_v[:, :PIECE], ALU.mult)
-        nc.vector.tensor_tensor(prod[:, HALF : HALF + PIECE], acc[2][:, :PIECE], gate[:, HALF : HALF + PIECE], ALU.mult)
-        nc.vector.tensor_tensor(prod[:, HALF + PIECE : S - LAST], acc[3][:, : PIECE - LAST], gate[:, HALF + PIECE : S - LAST], ALU.mult)
-        nc.vector.tensor_tensor(prod[:, S - LAST :], acc[3][:, PIECE - LAST : PIECE], gate_v[:, PIECE:], ALU.mult)
-        for lo in range(0, HALF, PIECE):
-            nc.scalar.activation(res[:, lo : lo + PIECE], prod[:, lo : lo + PIECE], RELU)
-        nc.scalar.dma_start(out=out[:, :PIECE], in_=res[:, :PIECE])
-        nc.sync.dma_start(out=out[:, PIECE:HALF], in_=res[:, PIECE:HALF])
-        for lo in range(HALF, S, PIECE):
-            nc.vector.tensor_scalar_max(res[:, lo : lo + PIECE], prod[:, lo : lo + PIECE], 0.0)
-        nc.sync.dma_start(out=out[:, HALF:], in_=res[:, HALF:])
+        for lo, hi in ((128, 256), (256, 320)):
+            nc.vector.tensor_copy(gate[:, lo:hi], looked_up(lo, hi))
+        for lo, hi in ((0, 128), (128, 256), (256, 384), (384, 512)):
+            i, first = divmod(lo, PIECE)
+            nc.vector.tensor_tensor(prod[:, lo:hi], acc[i][:, first : first + hi - lo], gate[:, lo:hi], ALU.mult)
+        for lo, hi in ((0, 128), (128, 256)):
+            nc.scalar.activation(res[:, lo:hi], prod[:, lo:hi], RELU)
+        for lo, hi in ((256, 384), (384, 512)):
+            nc.vector.tensor_scalar_max(res[:, lo:hi], prod[:, lo:hi], 0.0)
+        nc.scalar.dma_start(out=out[:, 0:128], in_=res[:, 0:128])
+        nc.sync.dma_start(out=out[:, 128:256], in_=res[:, 128:256])
+        nc.sync.dma_start(out=out[:, 256:512], in_=res[:, 256:512])

from contextlib import ExitStack

import concourse.mybir as mybir

K, T, S, N, U = 1024, 2048, 512, 128, 1024
FLOPS = 2 * K * N * S

F32 = mybir.dt.float32
BF16 = mybir.dt.bfloat16
U32 = mybir.dt.uint32
U16 = mybir.dt.uint16
U8 = mybir.dt.uint8
FP8X4 = mybir.dt.float8_e4m3fn_x4
ALU = mybir.AluOpType
COPY = mybir.ActivationFunctionType.Copy
RELU = mybir.ActivationFunctionType.Relu

P = 128
PACK = 4
K_PASS = P * PACK
PASSES = K // K_PASS
HALF = S // 2
PIECE = 128
PIECES = S // PIECE
X_ON_SCALAR = 256
W_ON_SCALAR = 96
W_BYTES = PACK * N * 4


def tile_picked_relu_e_kernel(tc, xT, w1, scale, offs, task, out):
    nc = tc.nc
    with ExitStack() as ctx:
        keep = ctx.enter_context(tc.tile_pool(name="keep", bufs=1))
        tail = ctx.enter_context(tc.tile_pool(name="tail", bufs=1))
        psum = ctx.enter_context(tc.psum_pool(name="psum", bufs=1))

        offs_sb = keep.tile([P, S // 16], U16, name="offs_sb")
        task_sb = keep.tile([P, S // 16], U16, name="task_sb")
        x_rows = xT.rearrange("(z p j) t -> z j p t", z=PASSES, j=PACK)
        w_rows = w1.rearrange("(z p j) n -> z p j n", z=PASSES, j=PACK)
        x_pass = xT.rearrange("(z p j) t -> z p j t", z=PASSES, j=PACK)
        planes = {}
        for z, lo, hi, queue, row in ((0, 0, 1, nc.sync, None), (0, 3, PACK, nc.scalar, 4096), (0, 1, 3, nc.sync, None), (1, 0, 2, nc.sync, None)):
            group = keep.tile([P, hi - lo, T], F32, name="group_%d_%d" % (z, lo), align_bytes=256)
            queue.dma_start(out=group[:], in_=x_pass[z][:, lo:hi, :], max_dma_last_dim=row)
            if (z, lo) == (0, 0):
                nc.sync.dma_start(offs_sb[:], offs)
                nc.sync.dma_start(task_sb[:], task)
            for j in range(lo, hi):
                planes[z, j] = group[:, j - lo, :]
        for j in range(2, PACK):
            single = keep.tile([P, T], F32, name="plane_%d" % j, align_bytes=256)
            nc.sync.dma_start(out=single[:], in_=x_rows[PASSES - 1, j])
            planes[PASSES - 1, j] = single[:]
        w_raw = []
        for z in range(PASSES):
            w_raw.append(tail.tile([P, PACK, N], F32, name="w_raw_%d" % z, offset=z * W_BYTES, align_bytes=256))
            nc.sync.dma_start(out=w_raw[z][:], in_=w_rows[z])
        scale_sb = keep.tile([P, U], F32, name="scale_sb", align_bytes=256)
        nc.sync.dma_start(out=scale_sb[:], in_=scale)

        w_bf = [keep.tile([P, N, PACK], BF16, name="w_bf_%d" % z, align_bytes=64) for z in range(PASSES)]
        w_codes = [keep.tile([P, N], U32, name="w_codes_%d" % z, align_bytes=64) for z in range(PASSES)]
        w_scales = [keep.tile([P, N], U8, name="w_scales_%d" % z, align_bytes=64) for z in range(PASSES)]
        x_bf = [keep.tile([P, S, PACK], BF16, name="x_bf_%d" % z, align_bytes=64) for z in range(PASSES)]
        x_codes = {}
        x_scales = {}
        for z in range(PASSES):
            for h in range(2):
                if z == 0:
                    x_codes[z, h] = keep.tile([P, HALF], U32, name="x_codes_%d_%d" % (z, h), align_bytes=64)
                else:
                    x_codes[z, h] = tail.tile([P, HALF], U32, name="x_codes_%d_%d" % (z, h), offset=h * W_BYTES, align_bytes=64)
                x_scales[z, h] = keep.tile([P, HALF], U8, name="x_scales_%d_%d" % (z, h), align_bytes=64)

        def entries(lst, lo, hi):
            return lst[:, lo // 16 : hi // 16]

        def quantize(codes, scales, src):
            nc.vector.quantize_mx(out=codes[:].bitcast(FP8X4), scales=scales[:], in_=src.rearrange("p c j -> p (c j)"))

        def quantize_x(z, h):
            quantize(x_codes[z, h], x_scales[z, h], x_bf[z][:, h * HALF : (h + 1) * HALF, :])

        for z in range(PASSES):
            paired = PACK if z == 0 else 2
            upper = keep.tile([P, paired, HALF], F32, name="upper_%d" % z)
            for j in range(paired):
                nc.vector.tensor_copy(x_bf[z][:, :HALF, j], planes[z, j].indirect(entries(offs_sb, 0, HALF)))
                nc.scalar.activation(upper[:, j, :], planes[z, j].indirect(entries(offs_sb, HALF, S)), COPY)
            nc.scalar.copy(
                x_bf[z][:, HALF:, :paired].rearrange("p (c i) j -> p c j i", i=4),
                upper[:].rearrange("p j (c i) -> p c j i", i=4),
            )
            for j in range(paired, PACK):
                window = planes[z, j]
                on_vector = S - X_ON_SCALAR if j == PACK - 1 else S
                nc.vector.tensor_copy(x_bf[z][:, :on_vector, j], window.indirect(entries(offs_sb, 0, on_vector)))
                if on_vector < S:
                    dense = keep.tile([P, X_ON_SCALAR], BF16, name="dense")
                    nc.scalar.activation(dense[:], window.indirect(entries(offs_sb, on_vector, S)), COPY)
                    nc.vector.tensor_copy(x_bf[z][:, on_vector:, j], dense[:])
            if z == 0:
                for h in range(2):
                    quantize_x(z, h)

        def round_w(copy, z, lo, hi):
            copy(
                w_bf[z][:, lo:hi, :].rearrange("p (c i) j -> p c j i", i=4),
                w_raw[z][:, :, lo:hi].rearrange("p j (c i) -> p c j i", i=4),
            )

        def gpsimd_round(dst, src):
            nc.gpsimd.tensor_scalar(dst, src, 1.0, 0.0, ALU.mult, ALU.add)

        for z in range(PASSES):
            round_w(nc.scalar.copy, z, 0, W_ON_SCALAR)
        round_w(gpsimd_round, 0, W_ON_SCALAR, N)
        quantize(w_codes[0], w_scales[0], w_bf[0][:])
        round_w(nc.vector.tensor_copy, 1, W_ON_SCALAR, N)
        quantize_x(1, 0)
        quantize(w_codes[1], w_scales[1], w_bf[1][:])
        quantize_x(1, 1)

        acc = [psum.tile([P, 512], F32, name="acc_%d" % i) for i in range(PIECES)]
        for z in range(PASSES):
            for i in range(PIECES):
                h, lo = divmod(i * PIECE, HALF)
                nc.tensor.matmul_mx(
                    out=acc[i][:, :PIECE],
                    lhsT=w_codes[z][:].bitcast(FP8X4),
                    lhsT_scale=w_scales[z][:],
                    rhs=x_codes[z, h][:, lo : lo + PIECE].bitcast(FP8X4),
                    rhs_scale=x_scales[z, h][:, lo : lo + PIECE],
                    start=(z == 0),
                    stop=(z == PASSES - 1),
                )

        gate = keep.tile([P, S], F32, name="gate")
        prod = keep.tile([P, S], F32, name="prod")
        res = keep.tile([P, S], F32, name="res", align_bytes=256)

        def looked_up(lo, hi):
            return scale_sb[:].indirect(entries(task_sb, lo, hi))

        for lo, hi in ((0, 128), (320, 384), (384, 512)):
            nc.scalar.activation(gate[:, lo:hi], looked_up(lo, hi), COPY)
        for lo, hi in ((128, 256), (256, 320)):
            nc.vector.tensor_copy(gate[:, lo:hi], looked_up(lo, hi))
        for lo, hi in ((0, 128), (128, 256), (256, 384), (384, 512)):
            i, first = divmod(lo, PIECE)
            nc.vector.tensor_tensor(prod[:, lo:hi], acc[i][:, first : first + hi - lo], gate[:, lo:hi], ALU.mult)
        for lo, hi in ((0, 128), (128, 256)):
            nc.scalar.activation(res[:, lo:hi], prod[:, lo:hi], RELU)
        for lo, hi in ((256, 384), (384, 512)):
            nc.vector.tensor_scalar_max(res[:, lo:hi], prod[:, lo:hi], 0.0)
        nc.scalar.dma_start(out=out[:, 0:128], in_=res[:, 0:128])
        nc.sync.dma_start(out=out[:, 128:256], in_=res[:, 128:256])
        nc.sync.dma_start(out=out[:, 256:512], in_=res[:, 256:512])
